import numpy as np
import ml_dtypes


def mxq(x, axis, fmt="e4m3"):
    dtype, down = {"e4m3": (ml_dtypes.float8_e4m3fn, 7), "e5m2": (ml_dtypes.float8_e5m2, 14)}[fmt]
    v = np.moveaxis(np.asarray(x, np.float32).astype(ml_dtypes.bfloat16).astype(np.float64), axis, -1)
    blocks = v.reshape(v.shape[:-1] + (-1, 32))
    amax = np.abs(blocks).max(-1, keepdims=True)
    byte = np.maximum(np.where(amax > 0, np.frexp(amax)[1] - 1 + 127, 0) - down, 1)
    scale = np.exp2(byte - 127.0)
    codes = (blocks / scale).astype(np.float32).astype(dtype).astype(np.float64)
    return np.moveaxis((codes * scale).reshape(v.shape), -1, axis)


WIDE = False


def mx_kscale(k):
    if not WIDE:
        return np.ones(k)
    levels = np.array([10, -10, 5, -5, 0])
    if k % 512:
        return np.exp2(np.random.permutation(np.resize(levels, k // 32))).repeat(32)
    a = np.empty((k // 512, 16))
    for p in range(k // 512):
        a[p, :8] = np.random.permutation(np.resize(levels, 8))
        for g in range(8):
            far = levels[np.abs(levels - a[p, g]) >= 10]
            a[p, g + 8] = far[np.random.randint(len(far))]
    return np.exp2(a.ravel()).repeat(32)


def f64(x):
    return np.asarray(x).astype(np.float64)


def striped(idx):
    return np.tile(idx.reshape(-1, 16).T, (8, 1)).astype(np.uint16)


def unstriped(offs):
    return offs[:16].T.reshape(-1).astype(np.int64)


E2M1 = np.array([0.0, 0.5, 1.0, 1.5, 2.0, 3.0, 4.0, 6.0, -0.0, -0.5, -1.0, -1.5, -2.0, -3.0, -4.0, -6.0])


def pack_weight(w, fmt):
    k, n = w.shape
    w = f64(np.asarray(w, np.float32).astype(ml_dtypes.bfloat16)).reshape(k // 32, 32, n)
    amax = np.abs(w).max(1)
    if fmt == "e4m3":
        byte = np.frexp(amax)[1] - 1 + 127 - 7
    else:
        mant, ex = np.frexp(amax / 6.0)
        byte = np.where(mant > 0.5, ex, ex - 1) + 127
    byte = np.clip(np.where(amax > 0, byte, 1), 1, 254)
    scaled = (w * np.exp2(127.0 - byte)[:, None, :]).reshape(k, n).astype(np.float32)
    by_word = np.ascontiguousarray(scaled.reshape(k // 512, 128, 4, n).transpose(0, 1, 3, 2))
    if fmt == "e4m3":
        words = by_word.astype(ml_dtypes.float8_e4m3fn).view(np.uint8)
    else:
        c = by_word.astype(ml_dtypes.float4_e2m1fn).view(np.uint8) & 0xF
        words = (c[..., 0::2] | (c[..., 1::2] << 4)).reshape(k // 512, 128, 2 * n)
    return np.ascontiguousarray(words), np.ascontiguousarray(byte.astype(np.uint8).reshape(k // 512, 16, n))


def unpack_weight(words, scales, fmt):
    g, _, n = scales.shape
    words = np.ascontiguousarray(words).reshape(g, 128, n, -1)
    if fmt == "e4m3":
        vals = words.view(ml_dtypes.float8_e4m3fn).astype(np.float64)
    else:
        nib = np.empty((g, 128, n, 4), np.uint8)
        nib[..., 0::2] = words & 0xF
        nib[..., 1::2] = words >> 4
        vals = E2M1[nib]
    vals = vals * np.repeat(np.exp2(scales.astype(np.float64) - 127.0), 8, axis=1)[..., None]
    return vals.transpose(0, 1, 3, 2).reshape(g * 512, n)


def gelu(v):
    return 0.5 * v * (1.0 + np.tanh(np.sqrt(2.0 / np.pi) * (v + 0.044715 * v**3)))


def bf(x):
    return np.asarray(x, np.float32).astype(ml_dtypes.bfloat16)


def planes(Y):
    n, m = Y.shape
    b = f64(bf(Y)).reshape(n // 32, 32, m)
    amax = np.abs(b).max(1)
    byte = np.clip(np.where(amax > 0, np.frexp(amax)[1] - 1 + 127 - 7, 1), 1, 254)
    codes = (b * np.exp2(127.0 - byte)[:, None, :]).reshape(n, m).astype(np.float32).astype(ml_dtypes.float8_e4m3fn).view(np.uint8)
    words = codes.reshape(n // 512, 128, 4, m).transpose(0, 1, 3, 2)
    return np.ascontiguousarray(words), np.ascontiguousarray(byte.astype(np.uint8).reshape(n // 512, 16, m))


K, H, T, S, T2, P = 1536, 512, 2048, 1024, 2048, 1024

def setup_inputs():
    n = np.random.standard_normal
    s, u = mx_kscale(K)[:, None], mx_kscale(H)[:, None]
    tab_words, tab_scales = pack_weight(n((K, T)) * s, "e4m3")
    w4_words, w4_scales = pack_weight(n((K, H)) / np.sqrt(K) / s * u.T, "e2m1")
    gain = np.exp(0.8 * n(H))
    return {
        "tab_words": tab_words, "tab_scales": tab_scales,
        "w4_words": w4_words, "w4_scales": w4_scales,
        "b": (0.6 * n(H) * u[:, 0]).astype(np.float32),
        "page0": (n((H, T2)) * u).astype(np.float32),
        "usual": (0.7 * n(H) * u[:, 0]).astype(np.float32),
        "w2": (n((H, H)) / np.sqrt(H) / u * gain).astype(np.float32),
        "d": (n(H) * gain / u[:, 0]).astype(np.float32),
        "offs": striped(np.random.permutation(T)[:S]),
        "offs2": striped(np.random.permutation(T2)[:S]),
        "offs3": striped(np.random.permutation(T2)[:P]),
    }

def reference(tab_words, tab_scales, w4_words, w4_scales, b, page0, usual, w2, d, offs, offs2, offs3):
    v = unpack_weight(tab_words, tab_scales, "e4m3")[:, unstriped(offs)]
    w4 = unpack_weight(w4_words, w4_scales, "e2m1")
    h = (w4.T @ v) + f64(b)[:, None]
    page = f64(page0).copy()
    l2 = unstriped(offs2)
    page[:, l2] = np.maximum(page[:, l2], h)
    x = np.abs(page[:, unstriped(offs3)] - f64(usual)[:, None])
    w2q = mxq(f64(w2), 0, "e4m3")
    y = (w2q.T @ mxq(x, 0, "e4m3")) + f64(d)[:, None] * h
    words, scales = planes(y)
    return y, words, scales

@@ -1,0 +1,259 @@
+from contextlib import ExitStack
+
+import concourse.mybir as mybir
+
+K, H, T, S, T2 = 1536, 512, 2048, 1024, 2048
+FLOPS = 2 * K * H * S + 2 * H * H * S
+
+F32 = mybir.dt.float32
+BF16 = mybir.dt.bfloat16
+I32 = mybir.dt.int32
+U32 = mybir.dt.uint32
+U16 = mybir.dt.uint16
+U8 = mybir.dt.uint8
+FP8X4 = mybir.dt.float8_e4m3fn_x4
+FP4X4 = mybir.dt.float4_e2m1fn_x4
+ALU = mybir.AluOpType
+ACT = mybir.ActivationFunctionType
+
+P = 128
+PACK = 4
+PASSES = K // (P * PACK)
+QUADS = 4
+QUAD = 32
+BANK = 512
+CHUNK = 256
+CHUNKS = S // CHUNK
+LIST_ROWS = 16
+LIVE_SPAN = (QUADS - 1) * QUAD + PACK
+
+
+def tile_list_restock_depletion_features_kernel(
+    tc, tab_words, tab_scales, w4_words, w4_scales, b, page0, usual, w2, d, offs, offs2, offs3, out_0, out_1, out_2
+):
+    nc = tc.nc
+    with ExitStack() as ctx:
+        keep = ctx.enter_context(tc.tile_pool(name="keep", bufs=1))
+        psum = ctx.enter_context(tc.psum_pool(name="psum", bufs=8))
+
+        list1 = keep.tile([P, S // LIST_ROWS], U16, name="list1")
+        list2 = keep.tile([P, S // LIST_ROWS], U16, name="list2")
+        list3 = keep.tile([P, S // LIST_ROWS], U16, name="list3")
+
+        w4_raw = keep.tile([P, PASSES, H // 2], I32, name="w4_raw")
+        w4s_raw = keep.tile([P, PASSES, H], U8, name="w4s_raw")
+        w4_codes = keep.tile([P, PASSES, PACK, P], U16, name="w4_codes", align_bytes=64)
+        w4_plane = keep.tile([P, PASSES, PACK, P], U8, name="w4_plane", align_bytes=64)
+        tab_plane = keep.tile([P, T], U8, name="tab_plane", align_bytes=64)
+        tab = [keep.tile([P, T], I32, name=f"tab{a}", align_bytes=64) for a in range(PASSES)]
+        v_codes = [keep.tile([P, S], U32, name=f"v_codes{a}", align_bytes=64) for a in range(PASSES)]
+        v_plane = [keep.tile([P, S], U8, name=f"v_plane{a}", align_bytes=64) for a in range(PASSES)]
+        page = [keep.tile([P, T2], F32, name=f"page{t}", align_bytes=64) for t in range(PACK)]
+        b_col = keep.tile([P, PACK], F32, name="b_col")
+        usual_col = keep.tile([P, PACK], F32, name="usual_col")
+        d_col = keep.tile([P, PACK], F32, name="d_col")
+        w2_raw = keep.tile([P, PACK, H], F32, name="w2_raw")
+
+        nc.gpsimd.memset(w4s_raw[:].rearrange("p a c -> p (a c)").bitcast(I32), 0)
+        nc.gpsimd.memset(tab_plane[:].bitcast(I32), 0)
+        for a in range(1, PASSES):
+            nc.vector.memset(v_plane[a][:].bitcast(I32), 0)
+
+        def load_tab(a):
+            nc.sync.dma_start(out=tab[a][:], in_=tab_words[a].rearrange("p t i -> p (t i)").bitcast(I32))
+
+        page_rows = page0.rearrange("(p t) c -> p t c", t=PACK)
+
+        def load_page(t):
+            nc.sync.dma_start(out=page[t][:], in_=page_rows[:, t, :])
+
+        nc.sync.dma_start(out=w4_raw[:], in_=w4_words.bitcast(I32).rearrange("a p w -> p a w"))
+        nc.sync.dma_start(list1[:], offs)
+        for q in range(QUADS):
+            nc.sync.dma_start(
+                out=w4s_raw[QUAD * q : QUAD * q + PACK].bitcast(I32),
+                in_=w4_scales[:, PACK * q : PACK * (q + 1), :].bitcast(I32).rearrange("a r w -> r a w"),
+            )
+        for q in range(QUADS):
+            nc.sync.dma_start(
+                out=tab_plane[QUAD * q : QUAD * q + PACK * PASSES, :].bitcast(I32),
+                in_=tab_scales[:, PACK * q : PACK * (q + 1), :].bitcast(I32),
+            )
+        load_tab(0)
+        load_tab(1)
+        nc.sync.dma_start(list2[:], offs2)
+        for t in range(PACK - 1):
+            load_page(t)
+        load_tab(PASSES - 1)
+        load_page(PACK - 1)
+        nc.sync.dma_start(out=b_col[:], in_=b.rearrange("(p t) -> p t", t=PACK))
+        nc.sync.dma_start(out=usual_col[:], in_=usual.rearrange("(p t) -> p t", t=PACK))
+        nc.sync.dma_start(out=d_col[:], in_=d.rearrange("(p t) -> p t", t=PACK))
+        nc.sync.dma_start(list3[:], offs3)
+        nc.sync.dma_start(out=w2_raw[:], in_=w2.rearrange("(p j) c -> p j c", j=PACK))
+
+        nc.vector.tensor_copy(
+            out=w4_codes[:],
+            in_=w4_raw[:].bitcast(U16).rearrange("p a (q t) -> p a t q", t=PACK),
+        )
+        nc.vector.tensor_copy(out=w4_plane[:], in_=w4s_raw[:].rearrange("p a (q t) -> p a t q", t=PACK))
+
+        larger = [keep.tile([P, S], F32, name=f"larger{t}") for t in range(PACK)]
+
+        def gather_words(a):
+            nc.vector.tensor_copy(out=v_codes[a][:], in_=tab[a][:].bitcast(U32).indirect(list1[:]))
+
+        def fetch_standing(t):
+            nc.vector.tensor_copy(out=larger[t][:], in_=page[t][:].indirect(list2[:]))
+
+        gather_words(0)
+        gather_words(1)
+        nc.vector.tensor_copy(out=v_plane[0][:], in_=tab_plane[:].indirect(list1[:]))
+        for a in range(1, PASSES):
+            nc.scalar.dma_start(
+                out=v_plane[a][0:LIVE_SPAN, :].bitcast(I32),
+                in_=v_plane[0][PACK * a : PACK * a + LIVE_SPAN, :].bitcast(I32),
+            )
+        for t in range(PACK - 1):
+            fetch_standing(t)
+        gather_words(PASSES - 1)
+        fetch_standing(PACK - 1)
+
+        halves = S // BANK
+        acc = [[psum.tile([P, BANK], F32, name="bank") for u in range(halves)] for t in range(PACK)]
+        for a in range(PASSES):
+            for t in range(PACK):
+                for u in range(halves):
+                    cols = slice(u * BANK, (u + 1) * BANK)
+                    nc.tensor.matmul_mx(
+                        out=acc[t][u][:],
+                        lhsT=w4_codes[:, a, t, :].bitcast(FP4X4),
+                        lhsT_scale=w4_plane[:, a, t, :],
+                        rhs=v_codes[a][:, cols].bitcast(FP8X4),
+                        rhs_scale=v_plane[a][:, cols],
+                        start=(a == 0),
+                        stop=(a == PASSES - 1),
+                    )
+
+        for t in range(PACK):
+            for u in range(halves):
+                cols = slice(u * BANK, (u + 1) * BANK)
+                nc.vector.scalar_tensor_tensor(
+                    out=larger[t][:, cols],
+                    in0=acc[t][u][:],
+                    scalar=b_col[:, t : t + 1],
+                    in1=larger[t][:, cols],
+                    op0=ALU.add,
+                    op1=ALU.max,
+                )
+
+        h = [keep.tile([P, S], F32, name=f"h{t}") for t in range(PACK)]
+        dh = [keep.tile([P, PACK, CHUNK], F32, name=f"dh{c}") for c in range(CHUNKS)]
+        for t in range(PACK):
+            for u in range(halves):
+                nc.scalar.activation(
+                    out=h[t][:, u * BANK : (u + 1) * BANK], in_=acc[t][u][:], func=ACT.Identity, bias=b_col[:, t : t + 1]
+                )
+        for t in range(PACK):
+            for c in range(CHUNKS):
+                nc.scalar.activation(
+                    out=dh[c][:, t, :], in_=h[t][:, c * CHUNK : (c + 1) * CHUNK], func=ACT.Copy, scale=d_col[:, t : t + 1]
+                )
+
+        w2_grouped = keep.tile([P, PACK, P, PACK], BF16, name="w2_grouped", align_bytes=64)
+        w2_codes = keep.tile([P, H], U32, name="w2_codes", align_bytes=64)
+        w2_plane = keep.tile([P, H], U8, name="w2_plane", align_bytes=64)
+        nc.scalar.copy(out=w2_grouped[:], in_=w2_raw[:].rearrange("p j (m t) -> p t m j", t=PACK))
+
+        read_last = [keep.tile([P, CHUNK], F32, name=f"read_last{c}") for c in range(CHUNKS)]
+        read_whole = [keep.tile([P, S], F32, name=f"read_whole{t}") for t in range(PACK - 1)]
+        x_grouped = [keep.tile([P, CHUNK, PACK], BF16, name=f"x_grouped{c}", align_bytes=64) for c in range(CHUNKS)]
+
+        def put_back(t):
+            nc.vector.tensor_copy(out=page[t][:].indirect(list2[:]), in_=larger[t][:])
+
+        def distance(t, c, values):
+            nc.scalar.activation(
+                out=x_grouped[c][:, :, t], in_=values, func=ACT.Abs, scale=-1.0, bias=usual_col[:, t : t + 1]
+            )
+
+        def read_page(t):
+            nc.vector.tensor_copy(out=read_whole[t][:], in_=page[t][:].indirect(list3[:]))
+            for c in range(CHUNKS):
+                distance(t, c, read_whole[t][:, c * CHUNK : (c + 1) * CHUNK])
+
+        def read_last_page(c):
+            t = PACK - 1
+            per = CHUNK // LIST_ROWS
+            nc.vector.tensor_copy(out=read_last[c][:], in_=page[t][:].indirect(list3[:, c * per : (c + 1) * per]))
+            distance(t, c, read_last[c][:])
+
+        put_back(0)
+        put_back(1)
+        read_page(0)
+        put_back(2)
+        read_page(1)
+        read_page(2)
+        put_back(3)
+        nc.vector.quantize_mx(
+            out=w2_codes[:].bitcast(FP8X4), scales=w2_plane[:], in_=w2_grouped[:].rearrange("p t m j -> p (t m j)")
+        )
+
+        x_codes = [keep.tile([P, CHUNK], U32, name=f"x_codes{c}", align_bytes=64) for c in range(CHUNKS)]
+        x_plane = [keep.tile([P, CHUNK], U8, name=f"x_plane{c}", align_bytes=64) for c in range(CHUNKS)]
+        y = [keep.tile([P, PACK, CHUNK], F32, name=f"y{c}") for c in range(CHUNKS)]
+        y_grouped = [keep.tile([P, CHUNK, PACK], BF16, name=f"y_grouped{c}", align_bytes=64) for c in range(CHUNKS)]
+        y_codes = [keep.tile([P, CHUNK], I32, name=f"y_codes{c}", align_bytes=64) for c in range(CHUNKS)]
+        y_plane = keep.tile([P, S], U8, name="y_plane", align_bytes=64)
+        out_rows = out_0.rearrange("(p t) j -> p t j", t=PACK)
+        out_words = out_1[0].rearrange("p m t -> p (m t)").bitcast(I32)
+        per_bank = BANK // CHUNK
+
+        def multiply(c):
+            nc.vector.quantize_mx(
+                out=x_codes[c][:].bitcast(FP8X4), scales=x_plane[c][:], in_=x_grouped[c][:].rearrange("p j t -> p (j t)")
+            )
+            banks = [psum.tile([P, per_bank, CHUNK], F32, name="bank") for u in range(PACK // per_bank)]
+            for t in range(PACK):
+                nc.tensor.matmul_mx(
+                    out=banks[t // per_bank][:, t % per_bank, :],
+                    lhsT=w2_codes[:, t * P : (t + 1) * P].bitcast(FP8X4),
+                    lhsT_scale=w2_plane[:, t * P : (t + 1) * P],
+                    rhs=x_codes[c][:].bitcast(FP8X4),
+                    rhs_scale=x_plane[c][:],
+                    start=True,
+                    stop=True,
+                )
+            return banks
+
+        def finish(c, banks):
+            for u, bank in enumerate(banks):
+                rows = slice(u * per_bank, (u + 1) * per_bank)
+                nc.vector.tensor_tensor(out=y[c][:, rows, :], in0=bank[:], in1=dh[c][:, rows, :], op=ALU.add)
+            nc.sync.dma_start(out=out_rows[:, :, c * CHUNK : (c + 1) * CHUNK], in_=y[c][:])
+            nc.scalar.copy(out=y_grouped[c][:], in_=y[c][:].rearrange("p t j -> p j t"))
+
+        def store_planes(c):
+            cols = slice(c * CHUNK, (c + 1) * CHUNK)
+            nc.vector.quantize_mx(
+                out=y_codes[c][:].bitcast(FP8X4), scales=y_plane[:, cols], in_=y_grouped[c][:].rearrange("p j t -> p (j t)")
+            )
+            nc.sync.dma_start(out=out_words[:, cols], in_=y_codes[c][:])
+
+        products = {}
+        for step in range(CHUNKS + 3):
+            if step < CHUNKS:
+                read_last_page(step)
+            if 0 <= step - 1 < CHUNKS:
+                products[step - 1] = multiply(step - 1)
+            if 0 <= step - 2 < CHUNKS:
+                finish(step - 2, products[step - 2])
+            if 0 <= step - 3 < CHUNKS:
+                store_planes(step - 3)
+
+        for q in range(QUADS):
+            queue = nc.sync if q % 2 == 0 else nc.scalar
+            queue.dma_start(
+                out=out_2[0, PACK * q : PACK * (q + 1), :].bitcast(I32),
+                in_=y_plane[QUAD * q : QUAD * q + PACK, :].bitcast(I32),
+            )

@@ -24,6 +24,8 @@ QUAD = 32
 BANK = 512
 CHUNK = 256
 CHUNKS = S // CHUNK
+STRIP = BANK // PACK
+STRIPS = S // STRIP
 LIST_ROWS = 16
 LIVE_SPAN = (QUADS - 1) * QUAD + PACK
 
@@ -42,8 +44,8 @@ def tile_list_restock_depletion_features_kernel(
 
         w4_raw = keep.tile([P, PASSES, H // 2], I32, name="w4_raw")
         w4s_raw = keep.tile([P, PASSES, H], U8, name="w4s_raw")
-        w4_codes = keep.tile([P, PASSES, PACK, P], U16, name="w4_codes", align_bytes=64)
-        w4_plane = keep.tile([P, PASSES, PACK, P], U8, name="w4_plane", align_bytes=64)
+        w4_codes = keep.tile([P, PACK, PASSES, P], U16, name="w4_codes", align_bytes=64)
+        w4_plane = keep.tile([P, PACK, PASSES, P], U8, name="w4_plane", align_bytes=64)
         tab_plane = keep.tile([P, T], U8, name="tab_plane", align_bytes=64)
         tab = [keep.tile([P, T], I32, name=f"tab{a}", align_bytes=64) for a in range(PASSES)]
         v_codes = [keep.tile([P, S], U32, name=f"v_codes{a}", align_bytes=64) for a in range(PASSES)]
@@ -74,12 +76,12 @@ def tile_list_restock_depletion_features_kernel(
                 out=w4s_raw[QUAD * q : QUAD * q + PACK].bitcast(I32),
                 in_=w4_scales[:, PACK * q : PACK * (q + 1), :].bitcast(I32).rearrange("a r w -> r a w"),
             )
+        load_tab(0)
         for q in range(QUADS):
             nc.sync.dma_start(
                 out=tab_plane[QUAD * q : QUAD * q + PACK * PASSES, :].bitcast(I32),
                 in_=tab_scales[:, PACK * q : PACK * (q + 1), :].bitcast(I32),
             )
-        load_tab(0)
         load_tab(1)
         nc.sync.dma_start(list2[:], offs2)
         for t in range(PACK - 1):
@@ -92,12 +94,6 @@ def tile_list_restock_depletion_features_kernel(
         nc.sync.dma_start(list3[:], offs3)
         nc.sync.dma_start(out=w2_raw[:], in_=w2.rearrange("(p j) c -> p j c", j=PACK))
 
-        nc.vector.tensor_copy(
-            out=w4_codes[:],
-            in_=w4_raw[:].bitcast(U16).rearrange("p a (q t) -> p a t q", t=PACK),
-        )
-        nc.vector.tensor_copy(out=w4_plane[:], in_=w4s_raw[:].rearrange("p a (q t) -> p a t q", t=PACK))
-
         larger = [keep.tile([P, S], F32, name=f"larger{t}") for t in range(PACK)]
 
         def gather_words(a):
@@ -106,14 +102,20 @@ def tile_list_restock_depletion_features_kernel(
         def fetch_standing(t):
             nc.vector.tensor_copy(out=larger[t][:], in_=page[t][:].indirect(list2[:]))
 
+        nc.vector.tensor_copy(
+            out=w4_codes[:],
+            in_=w4_raw[:].bitcast(U16).rearrange("p a (q t) -> p t a q", t=PACK),
+        )
+        nc.vector.tensor_copy(out=w4_plane[:], in_=w4s_raw[:].rearrange("p a (q t) -> p t a q", t=PACK))
+
         gather_words(0)
-        gather_words(1)
         nc.vector.tensor_copy(out=v_plane[0][:], in_=tab_plane[:].indirect(list1[:]))
         for a in range(1, PASSES):
             nc.scalar.dma_start(
                 out=v_plane[a][0:LIVE_SPAN, :].bitcast(I32),
                 in_=v_plane[0][PACK * a : PACK * a + LIVE_SPAN, :].bitcast(I32),
             )
+        gather_words(1)
         for t in range(PACK - 1):
             fetch_standing(t)
         gather_words(PASSES - 1)
@@ -127,8 +129,8 @@ def tile_list_restock_depletion_features_kernel(
                     cols = slice(u * BANK, (u + 1) * BANK)
                     nc.tensor.matmul_mx(
                         out=acc[t][u][:],
-                        lhsT=w4_codes[:, a, t, :].bitcast(FP4X4),
-                        lhsT_scale=w4_plane[:, a, t, :],
+                        lhsT=w4_codes[:, t, a, :].bitcast(FP4X4),
+                        lhsT_scale=w4_plane[:, t, a, :],
                         rhs=v_codes[a][:, cols].bitcast(FP8X4),
                         rhs_scale=v_plane[a][:, cols],
                         start=(a == 0),
@@ -148,52 +150,53 @@ def tile_list_restock_depletion_features_kernel(
                 )
 
         h = [keep.tile([P, S], F32, name=f"h{t}") for t in range(PACK)]
-        dh = [keep.tile([P, PACK, CHUNK], F32, name=f"dh{c}") for c in range(CHUNKS)]
+        dh = keep.tile([P, STRIPS, PACK, STRIP], F32, name="dh")
         for t in range(PACK):
             for u in range(halves):
                 nc.scalar.activation(
                     out=h[t][:, u * BANK : (u + 1) * BANK], in_=acc[t][u][:], func=ACT.Identity, bias=b_col[:, t : t + 1]
                 )
         for t in range(PACK):
-            for c in range(CHUNKS):
-                nc.scalar.activation(
-                    out=dh[c][:, t, :], in_=h[t][:, c * CHUNK : (c + 1) * CHUNK], func=ACT.Copy, scale=d_col[:, t : t + 1]
-                )
+            nc.scalar.activation(
+                out=dh[:, :, t, :],
+                in_=h[t][:].rearrange("p (s j) -> p s j", j=STRIP),
+                func=ACT.Copy,
+                scale=d_col[:, t : t + 1],
+            )
 
         w2_grouped = keep.tile([P, PACK, P, PACK], BF16, name="w2_grouped", align_bytes=64)
         w2_codes = keep.tile([P, H], U32, name="w2_codes", align_bytes=64)
         w2_plane = keep.tile([P, H], U8, name="w2_plane", align_bytes=64)
-        nc.scalar.copy(out=w2_grouped[:], in_=w2_raw[:].rearrange("p j (m t) -> p t m j", t=PACK))
+        nc.scalar.copy(
+            out=w2_grouped[:].rearrange("p t m j -> p m j t"), in_=w2_raw[:].rearrange("p j (m t) -> p m j t", t=PACK)
+        )
 
-        read_last = [keep.tile([P, CHUNK], F32, name=f"read_last{c}") for c in range(CHUNKS)]
-        read_whole = [keep.tile([P, S], F32, name=f"read_whole{t}") for t in range(PACK - 1)]
+        read = [keep.tile([P, S], F32, name=f"read{t}") for t in range(PACK)]
         x_grouped = [keep.tile([P, CHUNK, PACK], BF16, name=f"x_grouped{c}", align_bytes=64) for c in range(CHUNKS)]
 
         def put_back(t):
             nc.vector.tensor_copy(out=page[t][:].indirect(list2[:]), in_=larger[t][:])
 
-        def distance(t, c, values):
-            nc.scalar.activation(
-                out=x_grouped[c][:, :, t], in_=values, func=ACT.Abs, scale=-1.0, bias=usual_col[:, t : t + 1]
-            )
-
-        def read_page(t):
-            nc.vector.tensor_copy(out=read_whole[t][:], in_=page[t][:].indirect(list3[:]))
-            for c in range(CHUNKS):
-                distance(t, c, read_whole[t][:, c * CHUNK : (c + 1) * CHUNK])
-
-        def read_last_page(c):
-            t = PACK - 1
+        def read_page(t, first, last):
             per = CHUNK // LIST_ROWS
-            nc.vector.tensor_copy(out=read_last[c][:], in_=page[t][:].indirect(list3[:, c * per : (c + 1) * per]))
-            distance(t, c, read_last[c][:])
+            nc.vector.tensor_copy(
+                out=read[t][:, first * CHUNK : last * CHUNK], in_=page[t][:].indirect(list3[:, first * per : last * per])
+            )
+            for c in range(first, last):
+                nc.scalar.activation(
+                    out=x_grouped[c][:, :, t],
+                    in_=read[t][:, c * CHUNK : (c + 1) * CHUNK],
+                    func=ACT.Abs,
+                    scale=-1.0,
+                    bias=usual_col[:, t : t + 1],
+                )
 
         put_back(0)
         put_back(1)
-        read_page(0)
+        read_page(0, 0, CHUNKS)
         put_back(2)
-        read_page(1)
-        read_page(2)
+        read_page(1, 0, CHUNKS)
+        read_page(2, 0, CHUNKS - 1)
         put_back(3)
         nc.vector.quantize_mx(
             out=w2_codes[:].bitcast(FP8X4), scales=w2_plane[:], in_=w2_grouped[:].rearrange("p t m j -> p (t m j)")
@@ -201,55 +204,62 @@ def tile_list_restock_depletion_features_kernel(
 
         x_codes = [keep.tile([P, CHUNK], U32, name=f"x_codes{c}", align_bytes=64) for c in range(CHUNKS)]
         x_plane = [keep.tile([P, CHUNK], U8, name=f"x_plane{c}", align_bytes=64) for c in range(CHUNKS)]
-        y = [keep.tile([P, PACK, CHUNK], F32, name=f"y{c}") for c in range(CHUNKS)]
-        y_grouped = [keep.tile([P, CHUNK, PACK], BF16, name=f"y_grouped{c}", align_bytes=64) for c in range(CHUNKS)]
+        y = [keep.tile([P, PACK, STRIP], F32, name=f"y{s}") for s in range(STRIPS)]
+        y_grouped = [keep.tile([P, STRIP, PACK], BF16, name=f"y_grouped{s}", align_bytes=64) for s in range(STRIPS)]
         y_codes = [keep.tile([P, CHUNK], I32, name=f"y_codes{c}", align_bytes=64) for c in range(CHUNKS)]
         y_plane = keep.tile([P, S], U8, name="y_plane", align_bytes=64)
         out_rows = out_0.rearrange("(p t) j -> p t j", t=PACK)
         out_words = out_1[0].rearrange("p m t -> p (m t)").bitcast(I32)
-        per_bank = BANK // CHUNK
+        per_chunk = CHUNK // STRIP
 
-        def multiply(c):
+        def quantize_x(c):
             nc.vector.quantize_mx(
                 out=x_codes[c][:].bitcast(FP8X4), scales=x_plane[c][:], in_=x_grouped[c][:].rearrange("p j t -> p (j t)")
             )
-            banks = [psum.tile([P, per_bank, CHUNK], F32, name="bank") for u in range(PACK // per_bank)]
+
+        def multiply_and_add(s):
+            c, part = divmod(s, per_chunk)
+            cols = slice(part * STRIP, (part + 1) * STRIP)
+            bank = psum.tile([P, PACK, STRIP], F32, name="bank")
             for t in range(PACK):
                 nc.tensor.matmul_mx(
-                    out=banks[t // per_bank][:, t % per_bank, :],
+                    out=bank[:, t, :],
                     lhsT=w2_codes[:, t * P : (t + 1) * P].bitcast(FP8X4),
                     lhsT_scale=w2_plane[:, t * P : (t + 1) * P],
-                    rhs=x_codes[c][:].bitcast(FP8X4),
-                    rhs_scale=x_plane[c][:],
+                    rhs=x_codes[c][:, cols].bitcast(FP8X4),
+                    rhs_scale=x_plane[c][:, cols],
                     start=True,
                     stop=True,
                 )
-            return banks
-
-        def finish(c, banks):
-            for u, bank in enumerate(banks):
-                rows = slice(u * per_bank, (u + 1) * per_bank)
-                nc.vector.tensor_tensor(out=y[c][:, rows, :], in0=bank[:], in1=dh[c][:, rows, :], op=ALU.add)
-            nc.sync.dma_start(out=out_rows[:, :, c * CHUNK : (c + 1) * CHUNK], in_=y[c][:])
-            nc.scalar.copy(out=y_grouped[c][:], in_=y[c][:].rearrange("p t j -> p j t"))
-
-        def store_planes(c):
-            cols = slice(c * CHUNK, (c + 1) * CHUNK)
-            nc.vector.quantize_mx(
-                out=y_codes[c][:].bitcast(FP8X4), scales=y_plane[:, cols], in_=y_grouped[c][:].rearrange("p j t -> p (j t)")
+            nc.vector.tensor_tensor(out=y[s][:], in0=bank[:], in1=dh[:, s], op=ALU.add)
+            nc.sync.dma_start(out=out_rows[:, :, s * STRIP : (s + 1) * STRIP], in_=y[s][:])
+            nc.scalar.copy(
+                out=y_grouped[s][:].rearrange("p (g i) t -> p g t i", i=PACK),
+                in_=y[s][:].rearrange("p t (g i) -> p g t i", i=PACK),
             )
-            nc.sync.dma_start(out=out_words[:, cols], in_=y_codes[c][:])
 
-        products = {}
-        for step in range(CHUNKS + 3):
-            if step < CHUNKS:
-                read_last_page(step)
-            if 0 <= step - 1 < CHUNKS:
-                products[step - 1] = multiply(step - 1)
-            if 0 <= step - 2 < CHUNKS:
-                finish(step - 2, products[step - 2])
-            if 0 <= step - 3 < CHUNKS:
-                store_planes(step - 3)
+        def quantize_y(s):
+            c, part = divmod(s, per_chunk)
+            nc.vector.quantize_mx(
+                out=y_codes[c][:, part * STRIP : (part + 1) * STRIP].bitcast(FP8X4),
+                scales=y_plane[:, s * STRIP : (s + 1) * STRIP],
+                in_=y_grouped[s][:].rearrange("p j t -> p (j t)"),
+            )
+            if part == per_chunk - 1:
+                nc.sync.dma_start(out=out_words[:, c * CHUNK : (c + 1) * CHUNK], in_=y_codes[c][:])
+
+        for c in range(CHUNKS):
+            read_page(PACK - 1, c, c + 1)
+            if c >= 2:
+                quantize_x(c - 2)
+        read_page(PACK - 2, CHUNKS - 1, CHUNKS)
+        for s in range(STRIPS + 2):
+            if s % per_chunk == 1 and s // per_chunk + 2 < CHUNKS:
+                quantize_x(s // per_chunk + 2)
+            if s < STRIPS:
+                multiply_and_add(s)
+            if s >= 2:
+                quantize_y(s - 2)
 
         for q in range(QUADS):
             queue = nc.sync if q % 2 == 0 else nc.scalar

from contextlib import ExitStack

import concourse.mybir as mybir

K, H, T, S, T2 = 1536, 512, 2048, 1024, 2048
FLOPS = 2 * K * H * S + 2 * H * H * S

F32 = mybir.dt.float32
BF16 = mybir.dt.bfloat16
I32 = mybir.dt.int32
U32 = mybir.dt.uint32
U16 = mybir.dt.uint16
U8 = mybir.dt.uint8
FP8X4 = mybir.dt.float8_e4m3fn_x4
FP4X4 = mybir.dt.float4_e2m1fn_x4
ALU = mybir.AluOpType
ACT = mybir.ActivationFunctionType

P = 128
PACK = 4
PASSES = K // (P * PACK)
QUADS = 4
QUAD = 32
BANK = 512
CHUNK = 256
CHUNKS = S // CHUNK
STRIP = BANK // PACK
STRIPS = S // STRIP
LIST_ROWS = 16
LIVE_SPAN = (QUADS - 1) * QUAD + PACK


def tile_list_restock_depletion_features_kernel(
    tc, tab_words, tab_scales, w4_words, w4_scales, b, page0, usual, w2, d, offs, offs2, offs3, out_0, out_1, out_2
):
    nc = tc.nc
    with ExitStack() as ctx:
        keep = ctx.enter_context(tc.tile_pool(name="keep", bufs=1))
        psum = ctx.enter_context(tc.psum_pool(name="psum", bufs=8))

        list1 = keep.tile([P, S // LIST_ROWS], U16, name="list1")
        list2 = keep.tile([P, S // LIST_ROWS], U16, name="list2")
        list3 = keep.tile([P, S // LIST_ROWS], U16, name="list3")

        w4_raw = keep.tile([P, PASSES, H // 2], I32, name="w4_raw")
        w4s_raw = keep.tile([P, PASSES, H], U8, name="w4s_raw")
        w4_codes = keep.tile([P, PACK, PASSES, P], U16, name="w4_codes", align_bytes=64)
        w4_plane = keep.tile([P, PACK, PASSES, P], U8, name="w4_plane", align_bytes=64)
        tab_plane = keep.tile([P, T], U8, name="tab_plane", align_bytes=64)
        tab = [keep.tile([P, T], I32, name=f"tab{a}", align_bytes=64) for a in range(PASSES)]
        v_codes = [keep.tile([P, S], U32, name=f"v_codes{a}", align_bytes=64) for a in range(PASSES)]
        v_plane = [keep.tile([P, S], U8, name=f"v_plane{a}", align_bytes=64) for a in range(PASSES)]
        page = [keep.tile([P, T2], F32, name=f"page{t}", align_bytes=64) for t in range(PACK)]
        b_col = keep.tile([P, PACK], F32, name="b_col")
        usual_col = keep.tile([P, PACK], F32, name="usual_col")
        d_col = keep.tile([P, PACK], F32, name="d_col")
        w2_raw = keep.tile([P, PACK, H], F32, name="w2_raw")

        nc.gpsimd.memset(w4s_raw[:].rearrange("p a c -> p (a c)").bitcast(I32), 0)
        nc.gpsimd.memset(tab_plane[:].bitcast(I32), 0)
        for a in range(1, PASSES):
            nc.vector.memset(v_plane[a][:].bitcast(I32), 0)

        def load_tab(a):
            nc.sync.dma_start(out=tab[a][:], in_=tab_words[a].rearrange("p t i -> p (t i)").bitcast(I32))

        page_rows = page0.rearrange("(p t) c -> p t c", t=PACK)

        def load_page(t):
            nc.sync.dma_start(out=page[t][:], in_=page_rows[:, t, :])

        nc.sync.dma_start(out=w4_raw[:], in_=w4_words.bitcast(I32).rearrange("a p w -> p a w"))
        nc.sync.dma_start(list1[:], offs)
        for q in range(QUADS):
            nc.sync.dma_start(
                out=w4s_raw[QUAD * q : QUAD * q + PACK].bitcast(I32),
                in_=w4_scales[:, PACK * q : PACK * (q + 1), :].bitcast(I32).rearrange("a r w -> r a w"),
            )
        load_tab(0)
        for q in range(QUADS):
            nc.sync.dma_start(
                out=tab_plane[QUAD * q : QUAD * q + PACK * PASSES, :].bitcast(I32),
                in_=tab_scales[:, PACK * q : PACK * (q + 1), :].bitcast(I32),
            )
        load_tab(1)
        nc.sync.dma_start(list2[:], offs2)
        for t in range(PACK - 1):
            load_page(t)
        load_tab(PASSES - 1)
        load_page(PACK - 1)
        nc.sync.dma_start(out=b_col[:], in_=b.rearrange("(p t) -> p t", t=PACK))
        nc.sync.dma_start(out=usual_col[:], in_=usual.rearrange("(p t) -> p t", t=PACK))
        nc.sync.dma_start(out=d_col[:], in_=d.rearrange("(p t) -> p t", t=PACK))
        nc.sync.dma_start(list3[:], offs3)
        nc.sync.dma_start(out=w2_raw[:], in_=w2.rearrange("(p j) c -> p j c", j=PACK))

        larger = [keep.tile([P, S], F32, name=f"larger{t}") for t in range(PACK)]

        def gather_words(a):
            nc.vector.tensor_copy(out=v_codes[a][:], in_=tab[a][:].bitcast(U32).indirect(list1[:]))

        def fetch_standing(t):
            nc.vector.tensor_copy(out=larger[t][:], in_=page[t][:].indirect(list2[:]))

        nc.vector.tensor_copy(
            out=w4_codes[:],
            in_=w4_raw[:].bitcast(U16).rearrange("p a (q t) -> p t a q", t=PACK),
        )
        nc.vector.tensor_copy(out=w4_plane[:], in_=w4s_raw[:].rearrange("p a (q t) -> p t a q", t=PACK))

        gather_words(0)
        nc.vector.tensor_copy(out=v_plane[0][:], in_=tab_plane[:].indirect(list1[:]))
        for a in range(1, PASSES):
            nc.scalar.dma_start(
                out=v_plane[a][0:LIVE_SPAN, :].bitcast(I32),
                in_=v_plane[0][PACK * a : PACK * a + LIVE_SPAN, :].bitcast(I32),
            )
        gather_words(1)
        for t in range(PACK - 1):
            fetch_standing(t)
        gather_words(PASSES - 1)
        fetch_standing(PACK - 1)

        halves = S // BANK
        acc = [[psum.tile([P, BANK], F32, name="bank") for u in range(halves)] for t in range(PACK)]
        for a in range(PASSES):
            for t in range(PACK):
                for u in range(halves):
                    cols = slice(u * BANK, (u + 1) * BANK)
                    nc.tensor.matmul_mx(
                        out=acc[t][u][:],
                        lhsT=w4_codes[:, t, a, :].bitcast(FP4X4),
                        lhsT_scale=w4_plane[:, t, a, :],
                        rhs=v_codes[a][:, cols].bitcast(FP8X4),
                        rhs_scale=v_plane[a][:, cols],
                        start=(a == 0),
                        stop=(a == PASSES - 1),
                    )

        for t in range(PACK):
            for u in range(halves):
                cols = slice(u * BANK, (u + 1) * BANK)
                nc.vector.scalar_tensor_tensor(
                    out=larger[t][:, cols],
                    in0=acc[t][u][:],
                    scalar=b_col[:, t : t + 1],
                    in1=larger[t][:, cols],
                    op0=ALU.add,
                    op1=ALU.max,
                )

        h = [keep.tile([P, S], F32, name=f"h{t}") for t in range(PACK)]
        dh = keep.tile([P, STRIPS, PACK, STRIP], F32, name="dh")
        for t in range(PACK):
            for u in range(halves):
                nc.scalar.activation(
                    out=h[t][:, u * BANK : (u + 1) * BANK], in_=acc[t][u][:], func=ACT.Identity, bias=b_col[:, t : t + 1]
                )
        for t in range(PACK):
            nc.scalar.activation(
                out=dh[:, :, t, :],
                in_=h[t][:].rearrange("p (s j) -> p s j", j=STRIP),
                func=ACT.Copy,
                scale=d_col[:, t : t + 1],
            )

        w2_grouped = keep.tile([P, PACK, P, PACK], BF16, name="w2_grouped", align_bytes=64)
        w2_codes = keep.tile([P, H], U32, name="w2_codes", align_bytes=64)
        w2_plane = keep.tile([P, H], U8, name="w2_plane", align_bytes=64)
        nc.scalar.copy(
            out=w2_grouped[:].rearrange("p t m j -> p m j t"), in_=w2_raw[:].rearrange("p j (m t) -> p m j t", t=PACK)
        )

        read = [keep.tile([P, S], F32, name=f"read{t}") for t in range(PACK)]
        x_grouped = [keep.tile([P, CHUNK, PACK], BF16, name=f"x_grouped{c}", align_bytes=64) for c in range(CHUNKS)]

        def put_back(t):
            nc.vector.tensor_copy(out=page[t][:].indirect(list2[:]), in_=larger[t][:])

        def read_page(t, first, last):
            per = CHUNK // LIST_ROWS
            nc.vector.tensor_copy(
                out=read[t][:, first * CHUNK : last * CHUNK], in_=page[t][:].indirect(list3[:, first * per : last * per])
            )
            for c in range(first, last):
                nc.scalar.activation(
                    out=x_grouped[c][:, :, t],
                    in_=read[t][:, c * CHUNK : (c + 1) * CHUNK],
                    func=ACT.Abs,
                    scale=-1.0,
                    bias=usual_col[:, t : t + 1],
                )

        put_back(0)
        put_back(1)
        read_page(0, 0, CHUNKS)
        put_back(2)
        read_page(1, 0, CHUNKS)
        read_page(2, 0, CHUNKS - 1)
        put_back(3)
        nc.vector.quantize_mx(
            out=w2_codes[:].bitcast(FP8X4), scales=w2_plane[:], in_=w2_grouped[:].rearrange("p t m j -> p (t m j)")
        )

        x_codes = [keep.tile([P, CHUNK], U32, name=f"x_codes{c}", align_bytes=64) for c in range(CHUNKS)]
        x_plane = [keep.tile([P, CHUNK], U8, name=f"x_plane{c}", align_bytes=64) for c in range(CHUNKS)]
        y = [keep.tile([P, PACK, STRIP], F32, name=f"y{s}") for s in range(STRIPS)]
        y_grouped = [keep.tile([P, STRIP, PACK], BF16, name=f"y_grouped{s}", align_bytes=64) for s in range(STRIPS)]
        y_codes = [keep.tile([P, CHUNK], I32, name=f"y_codes{c}", align_bytes=64) for c in range(CHUNKS)]
        y_plane = keep.tile([P, S], U8, name="y_plane", align_bytes=64)
        out_rows = out_0.rearrange("(p t) j -> p t j", t=PACK)
        out_words = out_1[0].rearrange("p m t -> p (m t)").bitcast(I32)
        per_chunk = CHUNK // STRIP

        def quantize_x(c):
            nc.vector.quantize_mx(
                out=x_codes[c][:].bitcast(FP8X4), scales=x_plane[c][:], in_=x_grouped[c][:].rearrange("p j t -> p (j t)")
            )

        def multiply_and_add(s):
            c, part = divmod(s, per_chunk)
            cols = slice(part * STRIP, (part + 1) * STRIP)
            bank = psum.tile([P, PACK, STRIP], F32, name="bank")
            for t in range(PACK):
                nc.tensor.matmul_mx(
                    out=bank[:, t, :],
                    lhsT=w2_codes[:, t * P : (t + 1) * P].bitcast(FP8X4),
                    lhsT_scale=w2_plane[:, t * P : (t + 1) * P],
                    rhs=x_codes[c][:, cols].bitcast(FP8X4),
                    rhs_scale=x_plane[c][:, cols],
                    start=True,
                    stop=True,
                )
            nc.vector.tensor_tensor(out=y[s][:], in0=bank[:], in1=dh[:, s], op=ALU.add)
            nc.sync.dma_start(out=out_rows[:, :, s * STRIP : (s + 1) * STRIP], in_=y[s][:])
            nc.scalar.copy(
                out=y_grouped[s][:].rearrange("p (g i) t -> p g t i", i=PACK),
                in_=y[s][:].rearrange("p t (g i) -> p g t i", i=PACK),
            )

        def quantize_y(s):
            c, part = divmod(s, per_chunk)
            nc.vector.quantize_mx(
                out=y_codes[c][:, part * STRIP : (part + 1) * STRIP].bitcast(FP8X4),
                scales=y_plane[:, s * STRIP : (s + 1) * STRIP],
                in_=y_grouped[s][:].rearrange("p j t -> p (j t)"),
            )
            if part == per_chunk - 1:
                nc.sync.dma_start(out=out_words[:, c * CHUNK : (c + 1) * CHUNK], in_=y_codes[c][:])

        for c in range(CHUNKS):
            read_page(PACK - 1, c, c + 1)
            if c >= 2:
                quantize_x(c - 2)
        read_page(PACK - 2, CHUNKS - 1, CHUNKS)
        for s in range(STRIPS + 2):
            if s % per_chunk == 1 and s // per_chunk + 2 < CHUNKS:
                quantize_x(s // per_chunk + 2)
            if s < STRIPS:
                multiply_and_add(s)
            if s >= 2:
                quantize_y(s - 2)

        for q in range(QUADS):
            queue = nc.sync if q % 2 == 0 else nc.scalar
            queue.dma_start(
                out=out_2[0, PACK * q : PACK * (q + 1), :].bitcast(I32),
                in_=y_plane[QUAD * q : QUAD * q + PACK, :].bitcast(I32),
            )
